import numpy as np
import ml_dtypes


def mxq(x, axis, fmt="e4m3"):
    dtype, down = {"e4m3": (ml_dtypes.float8_e4m3fn, 7), "e5m2": (ml_dtypes.float8_e5m2, 14)}[fmt]
    v = np.moveaxis(np.asarray(x, np.float32).astype(ml_dtypes.bfloat16).astype(np.float64), axis, -1)
    blocks = v.reshape(v.shape[:-1] + (-1, 32))
    amax = np.abs(blocks).max(-1, keepdims=True)
    byte = np.maximum(np.where(amax > 0, np.frexp(amax)[1] - 1 + 127, 0) - down, 1)
    scale = np.exp2(byte - 127.0)
    codes = (blocks / scale).astype(np.float32).astype(dtype).astype(np.float64)
    return np.moveaxis((codes * scale).reshape(v.shape), -1, axis)


WIDE = False


def mx_kscale(k):
    if not WIDE:
        return np.ones(k)
    levels = np.array([10, -10, 5, -5, 0])
    if k % 512:
        return np.exp2(np.random.permutation(np.resize(levels, k // 32))).repeat(32)
    a = np.empty((k // 512, 16))
    for p in range(k // 512):
        a[p, :8] = np.random.permutation(np.resize(levels, 8))
        for g in range(8):
            far = levels[np.abs(levels - a[p, g]) >= 10]
            a[p, g + 8] = far[np.random.randint(len(far))]
    return np.exp2(a.ravel()).repeat(32)


def f64(x):
    return np.asarray(x).astype(np.float64)


def striped(idx):
    return np.tile(idx.reshape(-1, 16).T, (8, 1)).astype(np.uint16)


def unstriped(offs):
    return offs[:16].T.reshape(-1).astype(np.int64)


E2M1 = np.array([0.0, 0.5, 1.0, 1.5, 2.0, 3.0, 4.0, 6.0, -0.0, -0.5, -1.0, -1.5, -2.0, -3.0, -4.0, -6.0])


def pack_weight(w, fmt):
    k, n = w.shape
    w = f64(np.asarray(w, np.float32).astype(ml_dtypes.bfloat16)).reshape(k // 32, 32, n)
    amax = np.abs(w).max(1)
    if fmt == "e4m3":
        byte = np.frexp(amax)[1] - 1 + 127 - 7
    else:
        mant, ex = np.frexp(amax / 6.0)
        byte = np.where(mant > 0.5, ex, ex - 1) + 127
    byte = np.clip(np.where(amax > 0, byte, 1), 1, 254)
    scaled = (w * np.exp2(127.0 - byte)[:, None, :]).reshape(k, n).astype(np.float32)
    by_word = np.ascontiguousarray(scaled.reshape(k // 512, 128, 4, n).transpose(0, 1, 3, 2))
    if fmt == "e4m3":
        words = by_word.astype(ml_dtypes.float8_e4m3fn).view(np.uint8)
    else:
        c = by_word.astype(ml_dtypes.float4_e2m1fn).view(np.uint8) & 0xF
        words = (c[..., 0::2] | (c[..., 1::2] << 4)).reshape(k // 512, 128, 2 * n)
    return np.ascontiguousarray(words), np.ascontiguousarray(byte.astype(np.uint8).reshape(k // 512, 16, n))


def unpack_weight(words, scales, fmt):
    g, _, n = scales.shape
    words = np.ascontiguousarray(words).reshape(g, 128, n, -1)
    if fmt == "e4m3":
        vals = words.view(ml_dtypes.float8_e4m3fn).astype(np.float64)
    else:
        nib = np.empty((g, 128, n, 4), np.uint8)
        nib[..., 0::2] = words & 0xF
        nib[..., 1::2] = words >> 4
        vals = E2M1[nib]
    vals = vals * np.repeat(np.exp2(scales.astype(np.float64) - 127.0), 8, axis=1)[..., None]
    return vals.transpose(0, 1, 3, 2).reshape(g * 512, n)


def gelu(v):
    return 0.5 * v * (1.0 + np.tanh(np.sqrt(2.0 / np.pi) * (v + 0.044715 * v**3)))


K, K2, H, N, T, S = 1024, 512, 1024, 384, 4096, 1024


def setup_inputs():
    n = np.random.standard_normal
    s = mx_kscale(K)[:, None]
    s2 = mx_kscale(K2)[:, None]
    u = mx_kscale(H)[:, None]
    d = {}
    d["tab_words"], d["tab_scales"] = pack_weight(n((K, T)) * s, "e4m3")
    d["offs"] = striped(np.random.permutation(T)[:S])
    d["xs_words"], d["xs_scales"] = pack_weight(n((K2, S)) * s2, "e4m3")
    d["w1"] = (n((K, H)) / s / K**0.5).astype(np.float32)
    d["w2_words"], d["w2_scales"] = pack_weight(n((K, H)) / s * u.T / K**0.5, "e2m1")
    d["w3"] = (n((K2, H)) / s2 / K2**0.5).astype(np.float32)
    d["b1"] = (0.5 * n(H)).astype(np.float32)
    d["w4"] = (1.3 * n((H, N)) / u / H**0.5).astype(np.float32)
    d["b4"] = (0.6 * n(N)).astype(np.float32)
    return d


def reference(tab_words, tab_scales, offs, xs_words, xs_scales, w1, w2_words, w2_scales, w3, b1, w4, b4):
    v = unpack_weight(tab_words, tab_scales, "e4m3")[:, unstriped(offs)]
    xs = unpack_weight(xs_words, xs_scales, "e4m3")
    w2 = unpack_weight(w2_words, w2_scales, "e2m1")
    expected = mxq(f64(w1), 0, "e4m3").T @ v
    seen = mxq(f64(w3), 0, "e4m3").T @ xs
    weigh = w2.T @ v
    h = np.abs(expected - seen + f64(b1)[:, None]) * weigh
    y = mxq(f64(w4), 0, "e4m3").T @ mxq(h, 0, "e4m3")
    y = y + f64(b4)[:, None]
    return 1.0 / (1.0 + np.exp(-y))

@@ -1,0 +1,331 @@
+from contextlib import ExitStack
+
+import concourse.mybir as mybir
+from concourse.masks import make_identity
+
+K, K2, H, N, T, S = 1024, 512, 1024, 384, 4096, 1024
+FLOPS = 2 * S * (2 * K * H + K2 * H + H * N)
+
+F32 = mybir.dt.float32
+BF16 = mybir.dt.bfloat16
+I32 = mybir.dt.int32
+U32 = mybir.dt.uint32
+U16 = mybir.dt.uint16
+U8 = mybir.dt.uint8
+FP8X4 = mybir.dt.float8_e4m3fn_x4
+FP4X4 = mybir.dt.float4_e2m1fn_x4
+ACT = mybir.ActivationFunctionType
+ALU = mybir.AluOpType
+
+P = 128
+PACK = 4
+PASS = 512
+COLS = 512
+HALF = 256
+XS_ROW = 8
+
+
+def tile_list_signature_adjudication_scores_kernel(
+    tc, tab_words, tab_scales, offs, xs_words, xs_scales, w1, w2_words, w2_scales, w3, b1, w4, b4, out
+):
+    nc = tc.nc
+    with ExitStack() as ctx:
+        keep = ctx.enter_context(tc.tile_pool(name="keep", bufs=1))
+        stage = ctx.enter_context(tc.tile_pool(name="stage", bufs=4))
+        psum = ctx.enter_context(tc.psum_pool(name="psum", bufs=1))
+
+        def held(name, shape, dtype, tag=None):
+            return keep.tile(shape, dtype, name=name, tag=tag or name, align_bytes=64)
+
+        def bank(name, cols, number):
+            return psum.tile([P, cols], F32, name=name, tag="bank%d" % number)
+
+        offsets = keep.tile([P, S // 16], U16, name="offsets")
+        nc.sync.dma_start(offsets[:], offs)
+
+        w2_raw = held("w2_raw", [P, 2, H // 2], I32, "slot_x")
+        tab = [held("tab%d" % a, [P, T], I32) for a in range(2)]
+        nc.sync.dma_start(w2_raw[:], w2_words.bitcast(I32).rearrange("a p n -> p a n"))
+        for a in range(2):
+            nc.sync.dma_start(tab[a][:], tab_words[a].rearrange("p t i -> p (t i)").bitcast(I32))
+
+        tab_planes = held("tab_planes", [P, T], U8, "slot_a")
+        w2_planes_raw = held("w2_planes_raw", [P, 2 * H], U8, "slot_b")
+        v_plane1 = held("v_plane1", [P, S], U8)
+        xs_plane = held("xs_plane", [P, S], U8)
+        warm = held("warm", [P, 8], F32)
+        warm_out = held("warm_out", [P, 8], F32)
+        bias_rows = held("bias_rows", [P, 2 * P], F32)
+        identity = held("identity", [P, P], F32)
+        bias = held("bias", [P, 2, 8], F32)
+        make_identity(nc, identity[:])
+        nc.vector.memset(tab_planes[:].bitcast(I32), 0)
+        nc.vector.memset(w2_planes_raw[:].bitcast(I32), 0)
+        for q in range(4):
+            nc.scalar.dma_start(
+                tab_planes[32 * q : 32 * q + 8, :].bitcast(I32), tab_scales[:, 4 * q : 4 * q + 4, :].bitcast(I32)
+            )
+        for q in range(4):
+            nc.gpsimd.dma_start(
+                w2_planes_raw[32 * q : 32 * q + 4, :].bitcast(I32).rearrange("r (a n) -> r a n", a=2),
+                w2_scales[:, 4 * q : 4 * q + 4, :].bitcast(I32).rearrange("a r n -> r a n"),
+            )
+        nc.vector.memset(warm[:], 0.0)
+        nc.scalar.activation(warm_out[:], warm[:], ACT.Sigmoid)
+        nc.vector.memset(bias_rows[:], 0.0)
+        nc.vector.memset(v_plane1[:].bitcast(I32), 0)
+        nc.vector.memset(xs_plane[:].bitcast(I32), 0)
+        nc.gpsimd.dma_start(
+            bias_rows[0:PACK, :].rearrange("t (x q) -> t x q", q=8),
+            b1.rearrange("(x t q) -> t x q", t=PACK, q=8),
+        )
+        nc.gpsimd.dma_start(bias_rows[PACK : PACK + N // P, 0:P], b4.rearrange("(c p) -> c p", p=P))
+        for q in range(4):
+            nc.gpsimd.dma_start(
+                xs_plane[32 * q + XS_ROW : 32 * q + XS_ROW + 4, :].bitcast(I32),
+                xs_scales[0, 4 * q : 4 * q + 4, :].bitcast(I32),
+            )
+        turned = bank("turned", 2 * P, 7)
+        for b in range(2):
+            nc.tensor.transpose(turned[:, P * b : P * (b + 1)], bias_rows[:, P * b : P * (b + 1)], identity[:])
+        nc.scalar.copy(bias[:], turned[:].rearrange("p (b x) -> p b x", b=2)[:, :, 0:8])
+
+        w2_codes = held("w2_codes", [P, 4 * H], U8)
+        w2_planes = held("w2_planes", [P, 2 * H], U8)
+        v_planes = held("v_planes", [P, S], U8)
+        nc.vector.tensor_copy(
+            w2_codes[:].bitcast(I32).rearrange("p (x t g u) -> p x t g u", t=PACK, g=16, u=4),
+            w2_raw[:].rearrange("p a (b g t u) -> p (a b) t g u", t=PACK, g=16, u=4),
+        )
+        nc.vector.tensor_copy(v_planes[:], tab_planes[:].indirect(offsets[:]))
+        nc.scalar.dma_start(v_plane1[0:100, :].bitcast(I32), v_planes[4:104, :].bitcast(I32))
+        v_scale = [v_planes, v_plane1]
+        nc.vector.tensor_copy(
+            w2_planes[:].bitcast(I32).rearrange("p (x t g u) -> p x t g u", t=PACK, g=16, u=2),
+            w2_planes_raw[:].bitcast(I32).rearrange("p (x g t u) -> p x t g u", t=PACK, g=16, u=2),
+        )
+        v_codes = {(a, j): held("v_codes%d%d" % (a, j), [P, COLS], U32) for a in range(2) for j in range(2)}
+        for a in range(2):
+            for j in range(2):
+                nc.vector.tensor_copy(
+                    v_codes[a, j][:], tab[a][:].bitcast(U32).indirect(offsets[:, 32 * j : 32 * (j + 1)])
+                )
+
+        xs_codes = held("xs_codes", [P, S], I32, "slot_x")
+        nc.sync.dma_start(xs_codes[:], xs_words[0].rearrange("p c i -> p (c i)").bitcast(I32))
+
+        def load_weight(raw, w, a, b):
+            rows = w[PASS * a : PASS * (a + 1), PASS * b : PASS * (b + 1)]
+            nc.sync.dma_start(raw, rows.rearrange("(p j) c -> p j c", j=PACK))
+            return raw
+
+        single = [held("single%d" % i, [P, PACK, PASS], F32, "slot_" + "ab"[i]) for i in range(2)]
+        double = [held("double%d" % i, [P, 2, PACK, PASS], F32, "tab%d" % i) for i in range(2)]
+        w3_raw = {}
+        w1_raw = {}
+        w3_raw[0] = load_weight(single[0][:], w3, 0, 0)
+        w1_raw[0, 0] = load_weight(single[1][:], w1, 0, 0)
+        w1_raw[1, 0] = load_weight(double[0][:, 0], w1, 1, 0)
+        w3_raw[1] = load_weight(double[0][:, 1], w3, 0, 1)
+        w1_raw[0, 1] = load_weight(double[1][:, 0], w1, 0, 1)
+        w1_raw[1, 1] = load_weight(double[1][:, 1], w1, 1, 1)
+        w4_raw = {}
+
+        def load_w4(b):
+            w4_raw[b] = held("w4_raw%d" % b, [P, PACK, N], F32, "slot_" + "ab"[b])
+            rows = w4[PASS * b : PASS * (b + 1), :].rearrange("(g t q) n -> t g q n", t=PACK, q=8)
+            for t in range(PACK):
+                nc.sync.dma_start(w4_raw[b][:, t, :], rows[t])
+
+        weigh = {(b, j): held("weigh%d%d" % (b, j), [P, PACK * COLS], F32) for b in range(2) for j in range(2)}
+
+        def slot(tile, t):
+            return tile[:].rearrange("p (c t i) -> p t c i", t=PACK, i=4)[:, t]
+
+        def weigh_pass(acc, a, b, j, t):
+            m0 = H * a + PASS * b + P * t
+            nc.tensor.matmul_mx(
+                acc[:],
+                lhsT=w2_codes[:, 2 * m0 : 2 * (m0 + P)].bitcast(FP4X4),
+                lhsT_scale=w2_planes[:, m0 : m0 + P],
+                rhs=v_codes[a, j][:].bitcast(FP8X4),
+                rhs_scale=v_scale[a][:, COLS * j : COLS * (j + 1)],
+                start=(a == 0),
+                stop=(a == 1),
+            )
+
+        def weigh_out(acc, b, j, t):
+            nc.scalar.copy(slot(weigh[b, j], t), acc[:].rearrange("p (c i) -> p c i", i=4))
+
+        first = {(j, t): bank("weigh_first", COLS, PACK * j + t) for j in range(2) for t in range(PACK)}
+        for j in range(2):
+            for t in range(PACK):
+                weigh_pass(first[j, t], 0, 0, j, t)
+        for j in range(2):
+            for t in range(PACK):
+                weigh_pass(first[j, t], 1, 0, j, t)
+                weigh_out(first[j, t], 0, j, t)
+        for j in range(2):
+            for t in range(PACK):
+                acc = bank("weigh_acc", COLS, PACK * j + t)
+                weigh_pass(acc, 0, 1, j, t)
+                weigh_pass(acc, 1, 1, j, t)
+                weigh_out(acc, 1, j, t)
+
+        def quantise_weight(name, raw, negate, engines):
+            codes = held(name + "_codes", [P, PASS], U32)
+            plane = held(name + "_plane", [P, PASS], U8)
+            source = raw.rearrange("p j (g t q) -> p t g j q", t=PACK, q=8)
+            rounded = []
+            for u in range(2):
+                grouped = stage.tile([P, 2 * P * PACK], BF16, name="grouped", align_bytes=64)
+                target = grouped[:].rearrange("p (t g q j) -> p t g j q", t=2, q=8, j=PACK)
+                if negate:
+                    for t in range(2):
+                        if engines[u] == "v":
+                            nc.vector.tensor_scalar(target[:, t], source[:, 2 * u + t], -1.0, None, ALU.mult)
+                        else:
+                            nc.scalar.activation(target[:, t], source[:, 2 * u + t], ACT.Copy, scale=-1.0)
+                elif engines[u] == "v":
+                    nc.vector.tensor_copy(target, source[:, 2 * u : 2 * u + 2])
+                else:
+                    nc.scalar.copy(target, source[:, 2 * u : 2 * u + 2])
+                rounded.append(grouped)
+            for u in range(2):
+                cols = slice(2 * P * u, 2 * P * (u + 1))
+                nc.vector.quantize_mx(codes[:, cols].bitcast(FP8X4), plane[:, cols], rounded[u][:])
+            return codes, plane
+
+        def diff_pass(acc, weight, t, rhs, rhs_scale, first_pass, last_pass):
+            codes, plane = weight
+            nc.tensor.matmul_mx(
+                acc[:],
+                lhsT=codes[:, P * t : P * (t + 1)].bitcast(FP8X4),
+                lhsT_scale=plane[:, P * t : P * (t + 1)],
+                rhs=rhs.bitcast(FP8X4),
+                rhs_scale=rhs_scale,
+                start=first_pass,
+                stop=last_pass,
+            )
+
+        deviation = {}
+
+        def deviation_out(acc, b, j, t, c0, c1):
+            nc.scalar.activation(
+                slot(deviation[b, j], t)[:, c0 // 4 : c1 // 4],
+                acc[:, c0:c1].rearrange("p (c i) -> p c i", i=4),
+                ACT.Abs,
+                bias=bias[:, b, t : t + 1],
+            )
+
+        def first_stage(b, w3q, w1q0, w1q1):
+            for j in range(2):
+                deviation[b, j] = held("deviation%d%d" % (b, j), [P, PACK * COLS], F32)
+            accs = {(j, t): bank("diff_acc", COLS, PACK * j + t) for j in range(2) for t in range(PACK)}
+
+            def passes(j, t, which):
+                cols = slice(COLS * j, COLS * (j + 1))
+                if which == 0:
+                    diff_pass(accs[j, t], w3q, t, xs_codes[:, cols], xs_plane[XS_ROW:, cols], True, False)
+                elif which == 1:
+                    diff_pass(accs[j, t], w1q0, t, v_codes[0, j][:], v_scale[0][:, cols], False, False)
+                else:
+                    diff_pass(accs[j, t], w1q1, t, v_codes[1, j][:], v_scale[1][:, cols], False, True)
+
+            for which in range(3):
+                for t in range(PACK):
+                    passes(0, t, which)
+                    if which == 2:
+                        deviation_out(accs[0, t], b, 0, t, 0, COLS)
+            for t in range(PACK):
+                for which in range(3):
+                    passes(1, t, which)
+                if b == 0:
+                    deviation_out(accs[1, t], b, 1, t, 0, COLS)
+            if b == 1:
+                for u in range(2):
+                    for t in range(PACK):
+                        deviation_out(accs[1, t], b, 1, t, HALF * u, HALF * (u + 1))
+
+        h_codes = {(b, j): held("h_codes%d%d" % (b, j), [P, COLS], U32) for b in range(2) for j in range(2)}
+        h_plane = {(b, j): held("h_plane%d%d" % (b, j), [P, COLS], U8) for b in range(2) for j in range(2)}
+        h_rounded = {}
+
+        def multiply(b, j, u):
+            rounded = stage.tile([P, PACK * HALF], BF16, name="h_rounded", align_bytes=64)
+            part = slice(PACK * HALF * u, PACK * HALF * (u + 1))
+            nc.vector.tensor_tensor(
+                rounded[:].rearrange("p (c i t) -> p c t i", t=PACK, i=4),
+                deviation[b, j][:, part].rearrange("p (c t i) -> p c t i", t=PACK, i=4),
+                weigh[b, j][:, part].rearrange("p (c t i) -> p c t i", t=PACK, i=4),
+                ALU.mult,
+            )
+            h_rounded[b, j, u] = rounded
+
+        def quantise_h(b, j, u):
+            cols = slice(HALF * u, HALF * (u + 1))
+            nc.vector.quantize_mx(h_codes[b, j][:, cols].bitcast(FP8X4), h_plane[b, j][:, cols], h_rounded[b, j, u][:])
+
+        def make_h(b, j):
+            multiply(b, j, 0)
+            multiply(b, j, 1)
+            quantise_h(b, j, 0)
+            quantise_h(b, j, 1)
+
+        w4_codes = [held("w4_codes%d" % b, [P, N], U32) for b in range(2)]
+        w4_plane = [held("w4_plane%d" % b, [P, N], U8) for b in range(2)]
+
+        def quantise_w4(b, engines):
+            parts = ((0, 256), (256, 384))
+            rounded = []
+            for u, (n0, n1) in enumerate(parts):
+                grouped = stage.tile([P, PACK * (n1 - n0)], BF16, name="grouped", align_bytes=64)
+                target = grouped[:].rearrange("p (c i t) -> p c t i", t=PACK, i=4)
+                source = w4_raw[b][:, :, n0:n1].rearrange("p t (c i) -> p c t i", i=4)
+                if engines[u] == "v":
+                    nc.vector.tensor_copy(target, source)
+                else:
+                    nc.scalar.copy(target, source)
+                rounded.append(grouped)
+            for u, (n0, n1) in enumerate(parts):
+                nc.vector.quantize_mx(w4_codes[b][:, n0:n1].bitcast(FP8X4), w4_plane[b][:, n0:n1], rounded[u][:])
+
+        def second_stage(j, c0, c1, bank0):
+            for c in range(N // P):
+                acc = bank("score_acc", c1 - c0, (bank0 + c) % 8)
+                for b in range(2):
+                    nc.tensor.matmul_mx(
+                        acc[:],
+                        lhsT=w4_codes[b][:, P * c : P * (c + 1)].bitcast(FP8X4),
+                        lhsT_scale=w4_plane[b][:, P * c : P * (c + 1)],
+                        rhs=h_codes[b, j][:, c0:c1].bitcast(FP8X4),
+                        rhs_scale=h_plane[b, j][:, c0:c1],
+                        start=(b == 0),
+                        stop=(b == 1),
+                    )
+                scores = held("scores%d%d%d" % (j, c0, c), [P, c1 - c0], F32)
+                nc.scalar.activation(scores[:], acc[:], ACT.Sigmoid, bias=bias[:, 0, PACK + c : PACK + c + 1])
+                nc.sync.dma_start(out[P * c : P * (c + 1), COLS * j + c0 : COLS * j + c1], scores[:])
+
+        w3q = quantise_weight("w3_0", w3_raw[0], True, "vv")
+        load_w4(0)
+        w1q0 = quantise_weight("w1_00", w1_raw[0, 0], False, "vv")
+        load_w4(1)
+        w1q1 = quantise_weight("w1_10", w1_raw[1, 0], False, "vv")
+        first_stage(0, w3q, w1q0, w1q1)
+        w3q = quantise_weight("w3_1", w3_raw[1], True, "vv")
+        w1q0 = quantise_weight("w1_01", w1_raw[0, 1], False, "vv")
+        w1q1 = quantise_weight("w1_11", w1_raw[1, 1], False, "vs")
+        first_stage(1, w3q, w1q0, w1q1)
+        make_h(0, 0)
+        make_h(0, 1)
+        quantise_w4(0, "ss")
+        quantise_w4(1, "ss")
+        make_h(1, 0)
+        second_stage(0, 0, COLS, 0)
+        multiply(1, 1, 0)
+        multiply(1, 1, 1)
+        quantise_h(1, 1, 0)
+        second_stage(1, 0, HALF, 3)
+        quantise_h(1, 1, 1)
+        second_stage(1, HALF, COLS, 6)

@@ -43,11 +43,15 @@ def tile_list_signature_adjudication_scores_kernel(
         offsets = keep.tile([P, S // 16], U16, name="offsets")
         nc.sync.dma_start(offsets[:], offs)
 
-        w2_raw = held("w2_raw", [P, 2, H // 2], I32, "slot_x")
-        tab = [held("tab%d" % a, [P, T], I32) for a in range(2)]
+        w2_raw = held("w2_raw", [P, 2, H // 2], I32, "tab1")
         nc.sync.dma_start(w2_raw[:], w2_words.bitcast(I32).rearrange("a p n -> p a n"))
-        for a in range(2):
+        tab = {}
+
+        def load_tab(a):
+            tab[a] = held("tab%d" % a, [P, T], I32)
             nc.sync.dma_start(tab[a][:], tab_words[a].rearrange("p t i -> p (t i)").bitcast(I32))
+
+        load_tab(0)
 
         tab_planes = held("tab_planes", [P, T], U8, "slot_a")
         w2_planes_raw = held("w2_planes_raw", [P, 2 * H], U8, "slot_b")
@@ -61,12 +65,13 @@ def tile_list_signature_adjudication_scores_kernel(
         make_identity(nc, identity[:])
         nc.vector.memset(tab_planes[:].bitcast(I32), 0)
         nc.vector.memset(w2_planes_raw[:].bitcast(I32), 0)
-        for q in range(4):
+        for r in range(4):
             nc.scalar.dma_start(
-                tab_planes[32 * q : 32 * q + 8, :].bitcast(I32), tab_scales[:, 4 * q : 4 * q + 4, :].bitcast(I32)
+                tab_planes[r:P:16, :].bitcast(I32),
+                tab_scales.bitcast(I32).rearrange("a (q r) n -> r q a n", r=4)[r],
             )
         for q in range(4):
-            nc.gpsimd.dma_start(
+            (nc.scalar if q < 2 else nc.gpsimd).dma_start(
                 w2_planes_raw[32 * q : 32 * q + 4, :].bitcast(I32).rearrange("r (a n) -> r a n", a=2),
                 w2_scales[:, 4 * q : 4 * q + 4, :].bitcast(I32).rearrange("a r n -> r a n"),
             )
@@ -76,34 +81,31 @@ def tile_list_signature_adjudication_scores_kernel(
         nc.vector.memset(v_plane1[:].bitcast(I32), 0)
         nc.vector.memset(xs_plane[:].bitcast(I32), 0)
         nc.gpsimd.dma_start(
-            bias_rows[0:PACK, :].rearrange("t (x q) -> t x q", q=8),
-            b1.rearrange("(x t q) -> t x q", t=PACK, q=8),
+            bias_rows[0:PACK, :].rearrange("t (x i) -> t x i", i=4),
+            b1.rearrange("(x t i) -> t x i", t=PACK, i=4),
         )
         nc.gpsimd.dma_start(bias_rows[PACK : PACK + N // P, 0:P], b4.rearrange("(c p) -> c p", p=P))
         for q in range(4):
-            nc.gpsimd.dma_start(
+            nc.scalar.dma_start(
                 xs_plane[32 * q + XS_ROW : 32 * q + XS_ROW + 4, :].bitcast(I32),
                 xs_scales[0, 4 * q : 4 * q + 4, :].bitcast(I32),
             )
-        turned = bank("turned", 2 * P, 7)
-        for b in range(2):
-            nc.tensor.transpose(turned[:, P * b : P * (b + 1)], bias_rows[:, P * b : P * (b + 1)], identity[:])
-        nc.scalar.copy(bias[:], turned[:].rearrange("p (b x) -> p b x", b=2)[:, :, 0:8])
 
         w2_codes = held("w2_codes", [P, 4 * H], U8)
         w2_planes = held("w2_planes", [P, 2 * H], U8)
         v_planes = held("v_planes", [P, S], U8)
         nc.vector.tensor_copy(
-            w2_codes[:].bitcast(I32).rearrange("p (x t g u) -> p x t g u", t=PACK, g=16, u=4),
-            w2_raw[:].rearrange("p a (b g t u) -> p (a b) t g u", t=PACK, g=16, u=4),
+            w2_codes[:].bitcast(I32).rearrange("p (y t x u) -> p y t x u", t=PACK, x=32, u=2),
+            w2_raw[:].rearrange("p a (b x t u) -> p (a b) t x u", t=PACK, x=32, u=2),
+        )
+        load_tab(1)
+        nc.vector.tensor_copy(
+            w2_planes[:].bitcast(I32).rearrange("p (y t x) -> p y t x", t=PACK, x=32),
+            w2_planes_raw[:].bitcast(I32).rearrange("p (y x t) -> p y t x", t=PACK, x=32),
         )
         nc.vector.tensor_copy(v_planes[:], tab_planes[:].indirect(offsets[:]))
-        nc.scalar.dma_start(v_plane1[0:100, :].bitcast(I32), v_planes[4:104, :].bitcast(I32))
+        nc.scalar.dma_start(v_plane1[0:112, :].bitcast(I32), v_planes[16:P, :].bitcast(I32))
         v_scale = [v_planes, v_plane1]
-        nc.vector.tensor_copy(
-            w2_planes[:].bitcast(I32).rearrange("p (x t g u) -> p x t g u", t=PACK, g=16, u=2),
-            w2_planes_raw[:].bitcast(I32).rearrange("p (x g t u) -> p x t g u", t=PACK, g=16, u=2),
-        )
         v_codes = {(a, j): held("v_codes%d%d" % (a, j), [P, COLS], U32) for a in range(2) for j in range(2)}
         for a in range(2):
             for j in range(2):
@@ -111,7 +113,7 @@ def tile_list_signature_adjudication_scores_kernel(
                     v_codes[a, j][:], tab[a][:].bitcast(U32).indirect(offsets[:, 32 * j : 32 * (j + 1)])
                 )
 
-        xs_codes = held("xs_codes", [P, S], I32, "slot_x")
+        xs_codes = held("xs_codes", [P, S], I32, "slot_b")
         nc.sync.dma_start(xs_codes[:], xs_words[0].rearrange("p c i -> p (c i)").bitcast(I32))
 
         def load_weight(raw, w, a, b):
@@ -119,23 +121,25 @@ def tile_list_signature_adjudication_scores_kernel(
             nc.sync.dma_start(raw, rows.rearrange("(p j) c -> p j c", j=PACK))
             return raw
 
-        single = [held("single%d" % i, [P, PACK, PASS], F32, "slot_" + "ab"[i]) for i in range(2)]
+        early = held("early", [P, 2, PACK, PASS], F32, "slot_a")
         double = [held("double%d" % i, [P, 2, PACK, PASS], F32, "tab%d" % i) for i in range(2)]
         w3_raw = {}
         w1_raw = {}
-        w3_raw[0] = load_weight(single[0][:], w3, 0, 0)
-        w1_raw[0, 0] = load_weight(single[1][:], w1, 0, 0)
+        w3_raw[0] = load_weight(early[:, 0], w3, 0, 0)
+        w1_raw[0, 0] = load_weight(early[:, 1], w1, 0, 0)
         w1_raw[1, 0] = load_weight(double[0][:, 0], w1, 1, 0)
         w3_raw[1] = load_weight(double[0][:, 1], w3, 0, 1)
         w1_raw[0, 1] = load_weight(double[1][:, 0], w1, 0, 1)
         w1_raw[1, 1] = load_weight(double[1][:, 1], w1, 1, 1)
         w4_raw = {}
 
-        def load_w4(b):
-            w4_raw[b] = held("w4_raw%d" % b, [P, PACK, N], F32, "slot_" + "ab"[b])
-            rows = w4[PASS * b : PASS * (b + 1), :].rearrange("(g t q) n -> t g q n", t=PACK, q=8)
-            for t in range(PACK):
-                nc.sync.dma_start(w4_raw[b][:, t, :], rows[t])
+        def load_w4():
+            both = held("w4_raw", [P, 2, PACK, N], F32, "slot_a")
+            for b in range(2):
+                w4_raw[b] = both[:, b]
+                rows = w4[PASS * b : PASS * (b + 1), :].rearrange("(x t i) n -> t x i n", t=PACK, i=4)
+                for t in range(PACK):
+                    nc.sync.dma_start(both[:, b, t, :], rows[t])
 
         weigh = {(b, j): held("weigh%d%d" % (b, j), [P, PACK * COLS], F32) for b in range(2) for j in range(2)}
 
@@ -165,6 +169,10 @@ def tile_list_signature_adjudication_scores_kernel(
             for t in range(PACK):
                 weigh_pass(first[j, t], 1, 0, j, t)
                 weigh_out(first[j, t], 0, j, t)
+        turned = bank("turned", 2 * P, 7)
+        for b in range(2):
+            nc.tensor.transpose(turned[:, P * b : P * (b + 1)], bias_rows[:, P * b : P * (b + 1)], identity[:])
+        nc.scalar.copy(bias[:], turned[:].rearrange("p (b x) -> p b x", b=2)[:, :, 0:8])
         for j in range(2):
             for t in range(PACK):
                 acc = bank("weigh_acc", COLS, PACK * j + t)
@@ -175,11 +183,11 @@ def tile_list_signature_adjudication_scores_kernel(
         def quantise_weight(name, raw, negate, engines):
             codes = held(name + "_codes", [P, PASS], U32)
             plane = held(name + "_plane", [P, PASS], U8)
-            source = raw.rearrange("p j (g t q) -> p t g j q", t=PACK, q=8)
+            source = raw.rearrange("p j (x t i) -> p t x j i", t=PACK, i=4)
             rounded = []
             for u in range(2):
                 grouped = stage.tile([P, 2 * P * PACK], BF16, name="grouped", align_bytes=64)
-                target = grouped[:].rearrange("p (t g q j) -> p t g j q", t=2, q=8, j=PACK)
+                target = grouped[:].rearrange("p (t x i j) -> p t x j i", t=2, i=4, j=PACK)
                 if negate:
                     for t in range(2):
                         if engines[u] == "v":
@@ -308,9 +316,8 @@ def tile_list_signature_adjudication_scores_kernel(
                 nc.sync.dma_start(out[P * c : P * (c + 1), COLS * j + c0 : COLS * j + c1], scores[:])
 
         w3q = quantise_weight("w3_0", w3_raw[0], True, "vv")
-        load_w4(0)
         w1q0 = quantise_weight("w1_00", w1_raw[0, 0], False, "vv")
-        load_w4(1)
+        load_w4()
         w1q1 = quantise_weight("w1_10", w1_raw[1, 0], False, "vv")
         first_stage(0, w3q, w1q0, w1q1)
         w3q = quantise_weight("w3_1", w3_raw[1], True, "vv")

@@ -31,11 +31,15 @@ def tile_list_signature_adjudication_scores_kernel(
     nc = tc.nc
     with ExitStack() as ctx:
         keep = ctx.enter_context(tc.tile_pool(name="keep", bufs=1))
+        chain = ctx.enter_context(tc.tile_pool(name="chain", bufs=1))
         stage = ctx.enter_context(tc.tile_pool(name="stage", bufs=4))
         psum = ctx.enter_context(tc.psum_pool(name="psum", bufs=1))
 
         def held(name, shape, dtype, tag=None):
             return keep.tile(shape, dtype, name=name, tag=tag or name, align_bytes=64)
+
+        def placed(name, shape, dtype, kib):
+            return chain.tile(shape, dtype, name=name, align_bytes=64, offset=1024 * kib)
 
         def bank(name, cols, number):
             return psum.tile([P, cols], F32, name=name, tag="bank%d" % number)
@@ -53,8 +57,8 @@ def tile_list_signature_adjudication_scores_kernel(
 
         load_tab(0)
 
-        tab_planes = held("tab_planes", [P, T], U8, "slot_a")
-        w2_planes_raw = held("w2_planes_raw", [P, 2 * H], U8, "slot_b")
+        tab_planes = placed("tab_planes", [P, T], U8, 0)
+        w2_planes_raw = placed("w2_planes_raw", [P, 2 * H], U8, 20)
         v_plane1 = held("v_plane1", [P, S], U8)
         xs_plane = held("xs_plane", [P, S], U8)
         warm = held("warm", [P, 8], F32)
@@ -106,14 +110,16 @@ def tile_list_signature_adjudication_scores_kernel(
         nc.vector.tensor_copy(v_planes[:], tab_planes[:].indirect(offsets[:]))
         nc.scalar.dma_start(v_plane1[0:112, :].bitcast(I32), v_planes[16:P, :].bitcast(I32))
         v_scale = [v_planes, v_plane1]
-        v_codes = {(a, j): held("v_codes%d%d" % (a, j), [P, COLS], U32) for a in range(2) for j in range(2)}
+        v_codes = {(1, j): held("v_codes1%d" % j, [P, COLS], U32) for j in range(2)}
+        v_codes[0, 0] = placed("v_codes00", [P, COLS], U32, 0)
+        v_codes[0, 1] = placed("v_codes01", [P, COLS], U32, 19)
         for a in range(2):
             for j in range(2):
                 nc.vector.tensor_copy(
                     v_codes[a, j][:], tab[a][:].bitcast(U32).indirect(offsets[:, 32 * j : 32 * (j + 1)])
                 )
 
-        xs_codes = held("xs_codes", [P, S], I32, "slot_b")
+        xs_codes = placed("xs_codes", [P, S], I32, 21)
         nc.sync.dma_start(xs_codes[:], xs_words[0].rearrange("p c i -> p (c i)").bitcast(I32))
 
         def load_weight(raw, w, a, b):
@@ -121,7 +127,7 @@ def tile_list_signature_adjudication_scores_kernel(
             nc.sync.dma_start(raw, rows.rearrange("(p j) c -> p j c", j=PACK))
             return raw
 
-        early = held("early", [P, 2, PACK, PASS], F32, "slot_a")
+        early = placed("early", [P, 2, PACK, PASS], F32, 2)
         double = [held("double%d" % i, [P, 2, PACK, PASS], F32, "tab%d" % i) for i in range(2)]
         w3_raw = {}
         w1_raw = {}
@@ -134,7 +140,7 @@ def tile_list_signature_adjudication_scores_kernel(
         w4_raw = {}
 
         def load_w4():
-            both = held("w4_raw", [P, 2, PACK, N], F32, "slot_a")
+            both = placed("w4_raw", [P, 2, PACK, N], F32, 2)
             for b in range(2):
                 w4_raw[b] = both[:, b]
                 rows = w4[PASS * b : PASS * (b + 1), :].rearrange("(x t i) n -> t x i n", t=PACK, i=4)
@@ -183,21 +189,19 @@ def tile_list_signature_adjudication_scores_kernel(
         def quantise_weight(name, raw, negate, engines):
             codes = held(name + "_codes", [P, PASS], U32)
             plane = held(name + "_plane", [P, PASS], U8)
-            source = raw.rearrange("p j (x t i) -> p t x j i", t=PACK, i=4)
+            source = raw.rearrange("p j (x t h i) -> p t x h j i", t=PACK, h=2, i=2)
             rounded = []
             for u in range(2):
                 grouped = stage.tile([P, 2 * P * PACK], BF16, name="grouped", align_bytes=64)
-                target = grouped[:].rearrange("p (t x i j) -> p t x j i", t=2, i=4, j=PACK)
-                if negate:
-                    for t in range(2):
-                        if engines[u] == "v":
-                            nc.vector.tensor_scalar(target[:, t], source[:, 2 * u + t], -1.0, None, ALU.mult)
-                        else:
-                            nc.scalar.activation(target[:, t], source[:, 2 * u + t], ACT.Copy, scale=-1.0)
-                elif engines[u] == "v":
-                    nc.vector.tensor_copy(target, source[:, 2 * u : 2 * u + 2])
-                else:
-                    nc.scalar.copy(target, source[:, 2 * u : 2 * u + 2])
+                target = grouped[:].rearrange("p (t x h i j) -> p t x h j i", t=2, h=2, i=2, j=PACK)
+                for t in range(2):
+                    if negate:
+                        for h in range(2):
+                            nc.vector.tensor_scalar(target[:, t, :, h], source[:, 2 * u + t, :, h], -1.0, None, ALU.mult)
+                    elif engines[u] == "v":
+                        nc.vector.tensor_copy(target[:, t], source[:, 2 * u + t])
+                    else:
+                        nc.scalar.copy(target[:, t], source[:, 2 * u + t])
                 rounded.append(grouped)
             for u in range(2):
                 cols = slice(2 * P * u, 2 * P * (u + 1))
@@ -262,12 +266,13 @@ def tile_list_signature_adjudication_scores_kernel(
         def multiply(b, j, u):
             rounded = stage.tile([P, PACK * HALF], BF16, name="h_rounded", align_bytes=64)
             part = slice(PACK * HALF * u, PACK * HALF * (u + 1))
-            nc.vector.tensor_tensor(
-                rounded[:].rearrange("p (c i t) -> p c t i", t=PACK, i=4),
-                deviation[b, j][:, part].rearrange("p (c t i) -> p c t i", t=PACK, i=4),
-                weigh[b, j][:, part].rearrange("p (c t i) -> p c t i", t=PACK, i=4),
-                ALU.mult,
-            )
+            for h in range(2):
+                nc.vector.tensor_tensor(
+                    rounded[:].rearrange("p (c h i t) -> p h c t i", t=PACK, h=2, i=2)[:, h],
+                    deviation[b, j][:, part].rearrange("p (c t h i) -> p h c t i", t=PACK, h=2, i=2)[:, h],
+                    weigh[b, j][:, part].rearrange("p (c t h i) -> p h c t i", t=PACK, h=2, i=2)[:, h],
+                    ALU.mult,
+                )
             h_rounded[b, j, u] = rounded
 
         def quantise_h(b, j, u):
@@ -288,8 +293,8 @@ def tile_list_signature_adjudication_scores_kernel(
             rounded = []
             for u, (n0, n1) in enumerate(parts):
                 grouped = stage.tile([P, PACK * (n1 - n0)], BF16, name="grouped", align_bytes=64)
-                target = grouped[:].rearrange("p (c i t) -> p c t i", t=PACK, i=4)
-                source = w4_raw[b][:, :, n0:n1].rearrange("p t (c i) -> p c t i", i=4)
+                target = grouped[:].rearrange("p (c i t) -> p c t i", t=PACK, i=2)
+                source = w4_raw[b][:, :, n0:n1].rearrange("p t (c i) -> p c t i", i=2)
                 if engines[u] == "v":
                     nc.vector.tensor_copy(target, source)
                 else:

@@ -23,6 +23,7 @@ PASS = 512
 COLS = 512
 HALF = 256
 XS_ROW = 8
+TAB_ROW = 96
 
 
 def tile_list_signature_adjudication_scores_kernel(
@@ -47,19 +48,22 @@ def tile_list_signature_adjudication_scores_kernel(
         offsets = keep.tile([P, S // 16], U16, name="offsets")
         nc.sync.dma_start(offsets[:], offs)
 
-        w2_raw = held("w2_raw", [P, 2, H // 2], I32, "tab1")
+        tab_planes = placed("tab_planes", [P, T], U8, 3)
+        nc.sync.dma_start(
+            tab_planes[TAB_ROW:P, :].bitcast(I32), tab_scales.rearrange("a s n -> (a s) n").bitcast(I32)
+        )
+        w2_raw = held("w2_raw", [P, 2, H // 2], I32)
         nc.sync.dma_start(w2_raw[:], w2_words.bitcast(I32).rearrange("a p n -> p a n"))
         tab = {}
 
-        def load_tab(a):
-            tab[a] = held("tab%d" % a, [P, T], I32)
-            nc.sync.dma_start(tab[a][:], tab_words[a].rearrange("p t i -> p (t i)").bitcast(I32))
+        def load_tab(a, tile):
+            tab[a] = tile
+            nc.sync.dma_start(tile[:], tab_words[a].rearrange("p t i -> p (t i)").bitcast(I32))
 
-        load_tab(0)
+        load_tab(0, held("tab0", [P, T], I32))
 
-        tab_planes = placed("tab_planes", [P, T], U8, 0)
-        w2_planes_raw = placed("w2_planes_raw", [P, 2 * H], U8, 20)
-        v_plane1 = held("v_plane1", [P, S], U8)
+        w2_planes_raw = placed("w2_planes_raw", [P, 2 * H], U8, 32)
+        v_scale = [held("v_scale%d" % a, [P, S], U8) for a in range(2)]
         xs_plane = held("xs_plane", [P, S], U8)
         warm = held("warm", [P, 8], F32)
         warm_out = held("warm_out", [P, 8], F32)
@@ -67,59 +71,61 @@ def tile_list_signature_adjudication_scores_kernel(
         identity = held("identity", [P, P], F32)
         bias = held("bias", [P, 2, 8], F32)
         make_identity(nc, identity[:])
-        nc.vector.memset(tab_planes[:].bitcast(I32), 0)
         nc.vector.memset(w2_planes_raw[:].bitcast(I32), 0)
-        for r in range(4):
-            nc.scalar.dma_start(
-                tab_planes[r:P:16, :].bitcast(I32),
-                tab_scales.bitcast(I32).rearrange("a (q r) n -> r q a n", r=4)[r],
-            )
         for q in range(4):
-            (nc.scalar if q < 2 else nc.gpsimd).dma_start(
+            (nc.sync if q < 2 else nc.gpsimd).dma_start(
                 w2_planes_raw[32 * q : 32 * q + 4, :].bitcast(I32).rearrange("r (a n) -> r a n", a=2),
                 w2_scales[:, 4 * q : 4 * q + 4, :].bitcast(I32).rearrange("a r n -> r a n"),
             )
         nc.vector.memset(warm[:], 0.0)
         nc.scalar.activation(warm_out[:], warm[:], ACT.Sigmoid)
-        nc.vector.memset(bias_rows[:], 0.0)
-        nc.vector.memset(v_plane1[:].bitcast(I32), 0)
         nc.vector.memset(xs_plane[:].bitcast(I32), 0)
-        nc.gpsimd.dma_start(
-            bias_rows[0:PACK, :].rearrange("t (x i) -> t x i", i=4),
-            b1.rearrange("(x t i) -> t x i", t=PACK, i=4),
-        )
-        nc.gpsimd.dma_start(bias_rows[PACK : PACK + N // P, 0:P], b4.rearrange("(c p) -> c p", p=P))
+        nc.vector.memset(bias_rows[:], 0.0)
+        nc.vector.memset(tab_planes[0:TAB_ROW, :].bitcast(I32), 0)
+        for a in range(2):
+            nc.vector.memset(v_scale[a][:].bitcast(I32), 0)
         for q in range(4):
-            nc.scalar.dma_start(
+            nc.gpsimd.dma_start(
                 xs_plane[32 * q + XS_ROW : 32 * q + XS_ROW + 4, :].bitcast(I32),
                 xs_scales[0, 4 * q : 4 * q + 4, :].bitcast(I32),
             )
+        nc.gpsimd.dma_start(
+            bias_rows[0:PACK, :].rearrange("t (x q) -> t x q", q=8),
+            b1.rearrange("(x t q) -> t x q", t=PACK, q=8),
+        )
+        nc.gpsimd.dma_start(bias_rows[PACK : PACK + N // P, 0:P], b4.rearrange("(c p) -> c p", p=P))
 
         w2_codes = held("w2_codes", [P, 4 * H], U8)
-        w2_planes = held("w2_planes", [P, 2 * H], U8)
+        w2_planes = placed("w2_planes", [P, 2 * H], U8, 2)
         v_planes = held("v_planes", [P, S], U8)
-        nc.vector.tensor_copy(
-            w2_codes[:].bitcast(I32).rearrange("p (y t x u) -> p y t x u", t=PACK, x=32, u=2),
-            w2_raw[:].rearrange("p a (b x t u) -> p (a b) t x u", t=PACK, x=32, u=2),
-        )
-        load_tab(1)
-        nc.vector.tensor_copy(
-            w2_planes[:].bitcast(I32).rearrange("p (y t x) -> p y t x", t=PACK, x=32),
-            w2_planes_raw[:].bitcast(I32).rearrange("p (y x t) -> p y t x", t=PACK, x=32),
-        )
         nc.vector.tensor_copy(v_planes[:], tab_planes[:].indirect(offsets[:]))
-        nc.scalar.dma_start(v_plane1[0:112, :].bitcast(I32), v_planes[16:P, :].bitcast(I32))
-        v_scale = [v_planes, v_plane1]
-        v_codes = {(1, j): held("v_codes1%d" % j, [P, COLS], U32) for j in range(2)}
-        v_codes[0, 0] = placed("v_codes00", [P, COLS], U32, 0)
-        v_codes[0, 1] = placed("v_codes01", [P, COLS], U32, 19)
+
+        def deal_scale_rows(a):
+            for q in range(4):
+                row = TAB_ROW + 16 * a + 4 * q
+                nc.sync.dma_start(
+                    v_scale[a][32 * q : 32 * q + 4, :].bitcast(I32), v_planes[row : row + 4, :].bitcast(I32)
+                )
+
+        deal_scale_rows(0)
+        load_tab(1, placed("tab1", [P, T], I32, 6))
+        deal_scale_rows(1)
+        nc.vector.tensor_copy(
+            w2_codes[:].bitcast(I32).rearrange("p (y t g u) -> p y t g u", t=PACK, g=16, u=4),
+            w2_raw[:].rearrange("p a (b g t u) -> p (a b) t g u", t=PACK, g=16, u=4),
+        )
+        nc.vector.tensor_copy(
+            w2_planes[:].bitcast(I32).rearrange("p (y t g u) -> p y t g u", t=PACK, g=16, u=2),
+            w2_planes_raw[:].bitcast(I32).rearrange("p (y g t u) -> p y t g u", t=PACK, g=16, u=2),
+        )
+        v_codes = {(a, j): held("v_codes%d%d" % (a, j), [P, COLS], U32) for a in range(2) for j in range(2)}
         for a in range(2):
             for j in range(2):
                 nc.vector.tensor_copy(
                     v_codes[a, j][:], tab[a][:].bitcast(U32).indirect(offsets[:, 32 * j : 32 * (j + 1)])
                 )
 
-        xs_codes = placed("xs_codes", [P, S], I32, 21)
+        xs_codes = placed("xs_codes", [P, S], I32, 29)
         nc.sync.dma_start(xs_codes[:], xs_words[0].rearrange("p c i -> p (c i)").bitcast(I32))
 
         def load_weight(raw, w, a, b):
@@ -127,8 +133,8 @@ def tile_list_signature_adjudication_scores_kernel(
             nc.sync.dma_start(raw, rows.rearrange("(p j) c -> p j c", j=PACK))
             return raw
 
-        early = placed("early", [P, 2, PACK, PASS], F32, 2)
-        double = [held("double%d" % i, [P, 2, PACK, PASS], F32, "tab%d" % i) for i in range(2)]
+        early = placed("early", [P, 2, PACK, PASS], F32, 33)
+        double = [held("double0", [P, 2, PACK, PASS], F32, "tab0"), placed("double1", [P, 2, PACK, PASS], F32, 13)]
         w3_raw = {}
         w1_raw = {}
         w3_raw[0] = load_weight(early[:, 0], w3, 0, 0)
@@ -140,10 +146,10 @@ def tile_list_signature_adjudication_scores_kernel(
         w4_raw = {}
 
         def load_w4():
-            both = placed("w4_raw", [P, 2, PACK, N], F32, 2)
+            both = placed("w4_raw", [P, 2, PACK, N], F32, 33)
             for b in range(2):
                 w4_raw[b] = both[:, b]
-                rows = w4[PASS * b : PASS * (b + 1), :].rearrange("(x t i) n -> t x i n", t=PACK, i=4)
+                rows = w4[PASS * b : PASS * (b + 1), :].rearrange("(g t q) n -> t g q n", t=PACK, q=8)
                 for t in range(PACK):
                     nc.sync.dma_start(both[:, b, t, :], rows[t])
 
@@ -165,7 +171,10 @@ def tile_list_signature_adjudication_scores_kernel(
             )
 
         def weigh_out(acc, b, j, t):
-            nc.scalar.copy(slot(weigh[b, j], t), acc[:].rearrange("p (c i) -> p c i", i=4))
+            if (b, j) == (0, 0) and t >= 2:
+                nc.vector.tensor_copy(slot(weigh[b, j], t), acc[:].rearrange("p (c i) -> p c i", i=4))
+            else:
+                nc.scalar.copy(slot(weigh[b, j], t), acc[:].rearrange("p (c i) -> p c i", i=4))
 
         first = {(j, t): bank("weigh_first", COLS, PACK * j + t) for j in range(2) for t in range(PACK)}
         for j in range(2):
@@ -186,26 +195,25 @@ def tile_list_signature_adjudication_scores_kernel(
                 weigh_pass(acc, 1, 1, j, t)
                 weigh_out(acc, 1, j, t)
 
-        def quantise_weight(name, raw, negate, engines):
+        def quantise_weight(name, raw, negate, engines, staged):
             codes = held(name + "_codes", [P, PASS], U32)
             plane = held(name + "_plane", [P, PASS], U8)
-            source = raw.rearrange("p j (x t h i) -> p t x h j i", t=PACK, h=2, i=2)
+            source = raw.rearrange("p j (g t q) -> p t g j q", t=PACK, q=8)
             rounded = []
             for u in range(2):
-                grouped = stage.tile([P, 2 * P * PACK], BF16, name="grouped", align_bytes=64)
-                target = grouped[:].rearrange("p (t x h i j) -> p t x h j i", t=2, h=2, i=2, j=PACK)
-                for t in range(2):
-                    if negate:
-                        for h in range(2):
-                            nc.vector.tensor_scalar(target[:, t, :, h], source[:, 2 * u + t, :, h], -1.0, None, ALU.mult)
-                    elif engines[u] == "v":
-                        nc.vector.tensor_copy(target[:, t], source[:, 2 * u + t])
-                    else:
-                        nc.scalar.copy(target[:, t], source[:, 2 * u + t])
+                grouped = staged[:, 2 * P * PACK * u : 2 * P * PACK * (u + 1)]
+                target = grouped.rearrange("p (t g q j) -> p t g j q", t=2, q=8, j=PACK)
+                if negate:
+                    for t in range(2):
+                        nc.vector.tensor_scalar(target[:, t], source[:, 2 * u + t], -1.0, None, ALU.mult)
+                elif engines[u] == "v":
+                    nc.vector.tensor_copy(target, source[:, 2 * u : 2 * u + 2])
+                else:
+                    nc.scalar.copy(target, source[:, 2 * u : 2 * u + 2])
                 rounded.append(grouped)
             for u in range(2):
                 cols = slice(2 * P * u, 2 * P * (u + 1))
-                nc.vector.quantize_mx(codes[:, cols].bitcast(FP8X4), plane[:, cols], rounded[u][:])
+                nc.vector.quantize_mx(codes[:, cols].bitcast(FP8X4), plane[:, cols], rounded[u])
             return codes, plane
 
         def diff_pass(acc, weight, t, rhs, rhs_scale, first_pass, last_pass):
@@ -288,22 +296,24 @@ def tile_list_signature_adjudication_scores_kernel(
         w4_codes = [held("w4_codes%d" % b, [P, N], U32) for b in range(2)]
         w4_plane = [held("w4_plane%d" % b, [P, N], U8) for b in range(2)]
 
-        def quantise_w4(b, engines):
+        def quantise_w4(b, engines, staged):
             parts = ((0, 256), (256, 384))
             rounded = []
             for u, (n0, n1) in enumerate(parts):
-                grouped = stage.tile([P, PACK * (n1 - n0)], BF16, name="grouped", align_bytes=64)
-                target = grouped[:].rearrange("p (c i t) -> p c t i", t=PACK, i=2)
-                source = w4_raw[b][:, :, n0:n1].rearrange("p t (c i) -> p c t i", i=2)
+                grouped = staged[:, PACK * n0 : PACK * n1]
+                target = grouped.rearrange("p (c i t) -> p c t i", t=PACK, i=4)
+                source = w4_raw[b][:, :, n0:n1].rearrange("p t (c i) -> p c t i", i=4)
                 if engines[u] == "v":
                     nc.vector.tensor_copy(target, source)
                 else:
                     nc.scalar.copy(target, source)
                 rounded.append(grouped)
             for u, (n0, n1) in enumerate(parts):
-                nc.vector.quantize_mx(w4_codes[b][:, n0:n1].bitcast(FP8X4), w4_plane[b][:, n0:n1], rounded[u][:])
+                nc.vector.quantize_mx(w4_codes[b][:, n0:n1].bitcast(FP8X4), w4_plane[b][:, n0:n1], rounded[u])
 
         def second_stage(j, c0, c1, bank0):
+            scores = held("scores%d%d" % (j, c0), [P, N // P, c1 - c0], F32)
+            place = out[:, COLS * j + c0 : COLS * j + c1].rearrange("(c p) n -> p c n", p=P)
             for c in range(N // P):
                 acc = bank("score_acc", c1 - c0, (bank0 + c) % 8)
                 for b in range(2):
@@ -316,23 +326,23 @@ def tile_list_signature_adjudication_scores_kernel(
                         start=(b == 0),
                         stop=(b == 1),
                     )
-                scores = held("scores%d%d%d" % (j, c0, c), [P, c1 - c0], F32)
-                nc.scalar.activation(scores[:], acc[:], ACT.Sigmoid, bias=bias[:, 0, PACK + c : PACK + c + 1])
-                nc.sync.dma_start(out[P * c : P * (c + 1), COLS * j + c0 : COLS * j + c1], scores[:])
+                nc.scalar.activation(scores[:, c], acc[:], ACT.Sigmoid, bias=bias[:, 0, PACK + c : PACK + c + 1])
+                nc.sync.dma_start(place[:, c], scores[:, c])
 
-        w3q = quantise_weight("w3_0", w3_raw[0], True, "vv")
-        w1q0 = quantise_weight("w1_00", w1_raw[0, 0], False, "vv")
+        wide = [P, PACK * PASS]
+        w3q = quantise_weight("w3_0", w3_raw[0], True, "vv", placed("staged_a", wide, BF16, 5))
+        w1q0 = quantise_weight("w1_00", w1_raw[0, 0], False, "vv", placed("staged_b", wide, BF16, 9))
         load_w4()
-        w1q1 = quantise_weight("w1_10", w1_raw[1, 0], False, "vv")
+        w1q1 = quantise_weight("w1_10", w1_raw[1, 0], False, "vv", placed("staged_c", wide, BF16, 5))
         first_stage(0, w3q, w1q0, w1q1)
-        w3q = quantise_weight("w3_1", w3_raw[1], True, "vv")
-        w1q0 = quantise_weight("w1_01", w1_raw[0, 1], False, "vv")
-        w1q1 = quantise_weight("w1_11", w1_raw[1, 1], False, "vs")
-        first_stage(1, w3q, w1q0, w1q1)
+        w3q = quantise_weight("w3_1", w3_raw[1], True, "vv", placed("staged_d", wide, BF16, 9))
+        w1q0 = quantise_weight("w1_01", w1_raw[0, 1], False, "vv", placed("staged_e", wide, BF16, 5))
         make_h(0, 0)
+        w1q1 = quantise_weight("w1_11", w1_raw[1, 1], False, "vs", held("staged_f", wide, BF16, "deviation00"))
+        first_stage(1, w3q, w1q0, w1q1)
         make_h(0, 1)
-        quantise_w4(0, "ss")
-        quantise_w4(1, "ss")
+        quantise_w4(0, "ss", held("staged_g", [P, PACK * N], BF16, "weigh00"))
+        quantise_w4(1, "ss", held("staged_h", [P, PACK * N], BF16, "deviation01"))
         make_h(1, 0)
         second_stage(0, 0, COLS, 0)
         multiply(1, 1, 0)

from contextlib import ExitStack

import concourse.mybir as mybir
from concourse.masks import make_identity

K, K2, H, N, T, S = 1024, 512, 1024, 384, 4096, 1024
FLOPS = 2 * S * (2 * K * H + K2 * H + H * N)

F32 = mybir.dt.float32
BF16 = mybir.dt.bfloat16
I32 = mybir.dt.int32
U32 = mybir.dt.uint32
U16 = mybir.dt.uint16
U8 = mybir.dt.uint8
FP8X4 = mybir.dt.float8_e4m3fn_x4
FP4X4 = mybir.dt.float4_e2m1fn_x4
ACT = mybir.ActivationFunctionType
ALU = mybir.AluOpType

P = 128
PACK = 4
PASS = 512
COLS = 512
HALF = 256
XS_ROW = 8
TAB_ROW = 96


def tile_list_signature_adjudication_scores_kernel(
    tc, tab_words, tab_scales, offs, xs_words, xs_scales, w1, w2_words, w2_scales, w3, b1, w4, b4, out
):
    nc = tc.nc
    with ExitStack() as ctx:
        keep = ctx.enter_context(tc.tile_pool(name="keep", bufs=1))
        chain = ctx.enter_context(tc.tile_pool(name="chain", bufs=1))
        stage = ctx.enter_context(tc.tile_pool(name="stage", bufs=4))
        psum = ctx.enter_context(tc.psum_pool(name="psum", bufs=1))

        def held(name, shape, dtype, tag=None):
            return keep.tile(shape, dtype, name=name, tag=tag or name, align_bytes=64)

        def placed(name, shape, dtype, kib):
            return chain.tile(shape, dtype, name=name, align_bytes=64, offset=1024 * kib)

        def bank(name, cols, number):
            return psum.tile([P, cols], F32, name=name, tag="bank%d" % number)

        offsets = keep.tile([P, S // 16], U16, name="offsets")
        nc.sync.dma_start(offsets[:], offs)

        tab_planes = placed("tab_planes", [P, T], U8, 3)
        nc.sync.dma_start(
            tab_planes[TAB_ROW:P, :].bitcast(I32), tab_scales.rearrange("a s n -> (a s) n").bitcast(I32)
        )
        w2_raw = held("w2_raw", [P, 2, H // 2], I32)
        nc.sync.dma_start(w2_raw[:], w2_words.bitcast(I32).rearrange("a p n -> p a n"))
        tab = {}

        def load_tab(a, tile):
            tab[a] = tile
            nc.sync.dma_start(tile[:], tab_words[a].rearrange("p t i -> p (t i)").bitcast(I32))

        load_tab(0, held("tab0", [P, T], I32))

        w2_planes_raw = placed("w2_planes_raw", [P, 2 * H], U8, 32)
        v_scale = [held("v_scale%d" % a, [P, S], U8) for a in range(2)]
        xs_plane = held("xs_plane", [P, S], U8)
        warm = held("warm", [P, 8], F32)
        warm_out = held("warm_out", [P, 8], F32)
        bias_rows = held("bias_rows", [P, 2 * P], F32)
        identity = held("identity", [P, P], F32)
        bias = held("bias", [P, 2, 8], F32)
        make_identity(nc, identity[:])
        nc.vector.memset(w2_planes_raw[:].bitcast(I32), 0)
        for q in range(4):
            (nc.sync if q < 2 else nc.gpsimd).dma_start(
                w2_planes_raw[32 * q : 32 * q + 4, :].bitcast(I32).rearrange("r (a n) -> r a n", a=2),
                w2_scales[:, 4 * q : 4 * q + 4, :].bitcast(I32).rearrange("a r n -> r a n"),
            )
        nc.vector.memset(warm[:], 0.0)
        nc.scalar.activation(warm_out[:], warm[:], ACT.Sigmoid)
        nc.vector.memset(xs_plane[:].bitcast(I32), 0)
        nc.vector.memset(bias_rows[:], 0.0)
        nc.vector.memset(tab_planes[0:TAB_ROW, :].bitcast(I32), 0)
        for a in range(2):
            nc.vector.memset(v_scale[a][:].bitcast(I32), 0)
        for q in range(4):
            nc.gpsimd.dma_start(
                xs_plane[32 * q + XS_ROW : 32 * q + XS_ROW + 4, :].bitcast(I32),
                xs_scales[0, 4 * q : 4 * q + 4, :].bitcast(I32),
            )
        nc.gpsimd.dma_start(
            bias_rows[0:PACK, :].rearrange("t (x q) -> t x q", q=8),
            b1.rearrange("(x t q) -> t x q", t=PACK, q=8),
        )
        nc.gpsimd.dma_start(bias_rows[PACK : PACK + N // P, 0:P], b4.rearrange("(c p) -> c p", p=P))

        w2_codes = held("w2_codes", [P, 4 * H], U8)
        w2_planes = placed("w2_planes", [P, 2 * H], U8, 2)
        v_planes = held("v_planes", [P, S], U8)
        nc.vector.tensor_copy(v_planes[:], tab_planes[:].indirect(offsets[:]))

        def deal_scale_rows(a):
            for q in range(4):
                row = TAB_ROW + 16 * a + 4 * q
                nc.sync.dma_start(
                    v_scale[a][32 * q : 32 * q + 4, :].bitcast(I32), v_planes[row : row + 4, :].bitcast(I32)
                )

        deal_scale_rows(0)
        load_tab(1, placed("tab1", [P, T], I32, 6))
        deal_scale_rows(1)
        nc.vector.tensor_copy(
            w2_codes[:].bitcast(I32).rearrange("p (y t g u) -> p y t g u", t=PACK, g=16, u=4),
            w2_raw[:].rearrange("p a (b g t u) -> p (a b) t g u", t=PACK, g=16, u=4),
        )
        nc.vector.tensor_copy(
            w2_planes[:].bitcast(I32).rearrange("p (y t g u) -> p y t g u", t=PACK, g=16, u=2),
            w2_planes_raw[:].bitcast(I32).rearrange("p (y g t u) -> p y t g u", t=PACK, g=16, u=2),
        )
        v_codes = {(a, j): held("v_codes%d%d" % (a, j), [P, COLS], U32) for a in range(2) for j in range(2)}
        for a in range(2):
            for j in range(2):
                nc.vector.tensor_copy(
                    v_codes[a, j][:], tab[a][:].bitcast(U32).indirect(offsets[:, 32 * j : 32 * (j + 1)])
                )

        xs_codes = placed("xs_codes", [P, S], I32, 29)
        nc.sync.dma_start(xs_codes[:], xs_words[0].rearrange("p c i -> p (c i)").bitcast(I32))

        def load_weight(raw, w, a, b):
            rows = w[PASS * a : PASS * (a + 1), PASS * b : PASS * (b + 1)]
            nc.sync.dma_start(raw, rows.rearrange("(p j) c -> p j c", j=PACK))
            return raw

        early = placed("early", [P, 2, PACK, PASS], F32, 33)
        double = [held("double0", [P, 2, PACK, PASS], F32, "tab0"), placed("double1", [P, 2, PACK, PASS], F32, 13)]
        w3_raw = {}
        w1_raw = {}
        w3_raw[0] = load_weight(early[:, 0], w3, 0, 0)
        w1_raw[0, 0] = load_weight(early[:, 1], w1, 0, 0)
        w1_raw[1, 0] = load_weight(double[0][:, 0], w1, 1, 0)
        w3_raw[1] = load_weight(double[0][:, 1], w3, 0, 1)
        w1_raw[0, 1] = load_weight(double[1][:, 0], w1, 0, 1)
        w1_raw[1, 1] = load_weight(double[1][:, 1], w1, 1, 1)
        w4_raw = {}

        def load_w4():
            both = placed("w4_raw", [P, 2, PACK, N], F32, 33)
            for b in range(2):
                w4_raw[b] = both[:, b]
                rows = w4[PASS * b : PASS * (b + 1), :].rearrange("(g t q) n -> t g q n", t=PACK, q=8)
                for t in range(PACK):
                    nc.sync.dma_start(both[:, b, t, :], rows[t])

        weigh = {(b, j): held("weigh%d%d" % (b, j), [P, PACK * COLS], F32) for b in range(2) for j in range(2)}

        def slot(tile, t):
            return tile[:].rearrange("p (c t i) -> p t c i", t=PACK, i=4)[:, t]

        def weigh_pass(acc, a, b, j, t):
            m0 = H * a + PASS * b + P * t
            nc.tensor.matmul_mx(
                acc[:],
                lhsT=w2_codes[:, 2 * m0 : 2 * (m0 + P)].bitcast(FP4X4),
                lhsT_scale=w2_planes[:, m0 : m0 + P],
                rhs=v_codes[a, j][:].bitcast(FP8X4),
                rhs_scale=v_scale[a][:, COLS * j : COLS * (j + 1)],
                start=(a == 0),
                stop=(a == 1),
            )

        def weigh_out(acc, b, j, t):
            if (b, j) == (0, 0) and t >= 2:
                nc.vector.tensor_copy(slot(weigh[b, j], t), acc[:].rearrange("p (c i) -> p c i", i=4))
            else:
                nc.scalar.copy(slot(weigh[b, j], t), acc[:].rearrange("p (c i) -> p c i", i=4))

        first = {(j, t): bank("weigh_first", COLS, PACK * j + t) for j in range(2) for t in range(PACK)}
        for j in range(2):
            for t in range(PACK):
                weigh_pass(first[j, t], 0, 0, j, t)
        for j in range(2):
            for t in range(PACK):
                weigh_pass(first[j, t], 1, 0, j, t)
                weigh_out(first[j, t], 0, j, t)
        turned = bank("turned", 2 * P, 7)
        for b in range(2):
            nc.tensor.transpose(turned[:, P * b : P * (b + 1)], bias_rows[:, P * b : P * (b + 1)], identity[:])
        nc.scalar.copy(bias[:], turned[:].rearrange("p (b x) -> p b x", b=2)[:, :, 0:8])
        for j in range(2):
            for t in range(PACK):
                acc = bank("weigh_acc", COLS, PACK * j + t)
                weigh_pass(acc, 0, 1, j, t)
                weigh_pass(acc, 1, 1, j, t)
                weigh_out(acc, 1, j, t)

        def quantise_weight(name, raw, negate, engines, staged):
            codes = held(name + "_codes", [P, PASS], U32)
            plane = held(name + "_plane", [P, PASS], U8)
            source = raw.rearrange("p j (g t q) -> p t g j q", t=PACK, q=8)
            rounded = []
            for u in range(2):
                grouped = staged[:, 2 * P * PACK * u : 2 * P * PACK * (u + 1)]
                target = grouped.rearrange("p (t g q j) -> p t g j q", t=2, q=8, j=PACK)
                if negate:
                    for t in range(2):
                        nc.vector.tensor_scalar(target[:, t], source[:, 2 * u + t], -1.0, None, ALU.mult)
                elif engines[u] == "v":
                    nc.vector.tensor_copy(target, source[:, 2 * u : 2 * u + 2])
                else:
                    nc.scalar.copy(target, source[:, 2 * u : 2 * u + 2])
                rounded.append(grouped)
            for u in range(2):
                cols = slice(2 * P * u, 2 * P * (u + 1))
                nc.vector.quantize_mx(codes[:, cols].bitcast(FP8X4), plane[:, cols], rounded[u])
            return codes, plane

        def diff_pass(acc, weight, t, rhs, rhs_scale, first_pass, last_pass):
            codes, plane = weight
            nc.tensor.matmul_mx(
                acc[:],
                lhsT=codes[:, P * t : P * (t + 1)].bitcast(FP8X4),
                lhsT_scale=plane[:, P * t : P * (t + 1)],
                rhs=rhs.bitcast(FP8X4),
                rhs_scale=rhs_scale,
                start=first_pass,
                stop=last_pass,
            )

        deviation = {}

        def deviation_out(acc, b, j, t, c0, c1):
            nc.scalar.activation(
                slot(deviation[b, j], t)[:, c0 // 4 : c1 // 4],
                acc[:, c0:c1].rearrange("p (c i) -> p c i", i=4),
                ACT.Abs,
                bias=bias[:, b, t : t + 1],
            )

        def first_stage(b, w3q, w1q0, w1q1):
            for j in range(2):
                deviation[b, j] = held("deviation%d%d" % (b, j), [P, PACK * COLS], F32)
            accs = {(j, t): bank("diff_acc", COLS, PACK * j + t) for j in range(2) for t in range(PACK)}

            def passes(j, t, which):
                cols = slice(COLS * j, COLS * (j + 1))
                if which == 0:
                    diff_pass(accs[j, t], w3q, t, xs_codes[:, cols], xs_plane[XS_ROW:, cols], True, False)
                elif which == 1:
                    diff_pass(accs[j, t], w1q0, t, v_codes[0, j][:], v_scale[0][:, cols], False, False)
                else:
                    diff_pass(accs[j, t], w1q1, t, v_codes[1, j][:], v_scale[1][:, cols], False, True)

            for which in range(3):
                for t in range(PACK):
                    passes(0, t, which)
                    if which == 2:
                        deviation_out(accs[0, t], b, 0, t, 0, COLS)
            for t in range(PACK):
                for which in range(3):
                    passes(1, t, which)
                if b == 0:
                    deviation_out(accs[1, t], b, 1, t, 0, COLS)
            if b == 1:
                for u in range(2):
                    for t in range(PACK):
                        deviation_out(accs[1, t], b, 1, t, HALF * u, HALF * (u + 1))

        h_codes = {(b, j): held("h_codes%d%d" % (b, j), [P, COLS], U32) for b in range(2) for j in range(2)}
        h_plane = {(b, j): held("h_plane%d%d" % (b, j), [P, COLS], U8) for b in range(2) for j in range(2)}
        h_rounded = {}

        def multiply(b, j, u):
            rounded = stage.tile([P, PACK * HALF], BF16, name="h_rounded", align_bytes=64)
            part = slice(PACK * HALF * u, PACK * HALF * (u + 1))
            for h in range(2):
                nc.vector.tensor_tensor(
                    rounded[:].rearrange("p (c h i t) -> p h c t i", t=PACK, h=2, i=2)[:, h],
                    deviation[b, j][:, part].rearrange("p (c t h i) -> p h c t i", t=PACK, h=2, i=2)[:, h],
                    weigh[b, j][:, part].rearrange("p (c t h i) -> p h c t i", t=PACK, h=2, i=2)[:, h],
                    ALU.mult,
                )
            h_rounded[b, j, u] = rounded

        def quantise_h(b, j, u):
            cols = slice(HALF * u, HALF * (u + 1))
            nc.vector.quantize_mx(h_codes[b, j][:, cols].bitcast(FP8X4), h_plane[b, j][:, cols], h_rounded[b, j, u][:])

        def make_h(b, j):
            multiply(b, j, 0)
            multiply(b, j, 1)
            quantise_h(b, j, 0)
            quantise_h(b, j, 1)

        w4_codes = [held("w4_codes%d" % b, [P, N], U32) for b in range(2)]
        w4_plane = [held("w4_plane%d" % b, [P, N], U8) for b in range(2)]

        def quantise_w4(b, engines, staged):
            parts = ((0, 256), (256, 384))
            rounded = []
            for u, (n0, n1) in enumerate(parts):
                grouped = staged[:, PACK * n0 : PACK * n1]
                target = grouped.rearrange("p (c i t) -> p c t i", t=PACK, i=4)
                source = w4_raw[b][:, :, n0:n1].rearrange("p t (c i) -> p c t i", i=4)
                if engines[u] == "v":
                    nc.vector.tensor_copy(target, source)
                else:
                    nc.scalar.copy(target, source)
                rounded.append(grouped)
            for u, (n0, n1) in enumerate(parts):
                nc.vector.quantize_mx(w4_codes[b][:, n0:n1].bitcast(FP8X4), w4_plane[b][:, n0:n1], rounded[u])

        def second_stage(j, c0, c1, bank0):
            scores = held("scores%d%d" % (j, c0), [P, N // P, c1 - c0], F32)
            place = out[:, COLS * j + c0 : COLS * j + c1].rearrange("(c p) n -> p c n", p=P)
            for c in range(N // P):
                acc = bank("score_acc", c1 - c0, (bank0 + c) % 8)
                for b in range(2):
                    nc.tensor.matmul_mx(
                        acc[:],
                        lhsT=w4_codes[b][:, P * c : P * (c + 1)].bitcast(FP8X4),
                        lhsT_scale=w4_plane[b][:, P * c : P * (c + 1)],
                        rhs=h_codes[b, j][:, c0:c1].bitcast(FP8X4),
                        rhs_scale=h_plane[b, j][:, c0:c1],
                        start=(b == 0),
                        stop=(b == 1),
                    )
                nc.scalar.activation(scores[:, c], acc[:], ACT.Sigmoid, bias=bias[:, 0, PACK + c : PACK + c + 1])
                nc.sync.dma_start(place[:, c], scores[:, c])

        wide = [P, PACK * PASS]
        w3q = quantise_weight("w3_0", w3_raw[0], True, "vv", placed("staged_a", wide, BF16, 5))
        w1q0 = quantise_weight("w1_00", w1_raw[0, 0], False, "vv", placed("staged_b", wide, BF16, 9))
        load_w4()
        w1q1 = quantise_weight("w1_10", w1_raw[1, 0], False, "vv", placed("staged_c", wide, BF16, 5))
        first_stage(0, w3q, w1q0, w1q1)
        w3q = quantise_weight("w3_1", w3_raw[1], True, "vv", placed("staged_d", wide, BF16, 9))
        w1q0 = quantise_weight("w1_01", w1_raw[0, 1], False, "vv", placed("staged_e", wide, BF16, 5))
        make_h(0, 0)
        w1q1 = quantise_weight("w1_11", w1_raw[1, 1], False, "vs", held("staged_f", wide, BF16, "deviation00"))
        first_stage(1, w3q, w1q0, w1q1)
        make_h(0, 1)
        quantise_w4(0, "ss", held("staged_g", [P, PACK * N], BF16, "weigh00"))
        quantise_w4(1, "ss", held("staged_h", [P, PACK * N], BF16, "deviation01"))
        make_h(1, 0)
        second_stage(0, 0, COLS, 0)
        multiply(1, 1, 0)
        multiply(1, 1, 1)
        quantise_h(1, 1, 0)
        second_stage(1, 0, HALF, 3)
        quantise_h(1, 1, 1)
        second_stage(1, HALF, COLS, 6)
